import numpy as np
import ml_dtypes


def mxq(x, axis, fmt="e4m3"):
    dtype, down = {"e4m3": (ml_dtypes.float8_e4m3fn, 7), "e5m2": (ml_dtypes.float8_e5m2, 14)}[fmt]
    v = np.moveaxis(np.asarray(x, np.float32).astype(ml_dtypes.bfloat16).astype(np.float64), axis, -1)
    blocks = v.reshape(v.shape[:-1] + (-1, 32))
    amax = np.abs(blocks).max(-1, keepdims=True)
    byte = np.maximum(np.where(amax > 0, np.frexp(amax)[1] - 1 + 127, 0) - down, 1)
    scale = np.exp2(byte - 127.0)
    codes = (blocks / scale).astype(np.float32).astype(dtype).astype(np.float64)
    return np.moveaxis((codes * scale).reshape(v.shape), -1, axis)


WIDE = False


def mx_kscale(k):
    if not WIDE:
        return np.ones(k)
    levels = np.array([24, -24, 12, -12, 0])
    if k % 512:
        return np.exp2(np.random.permutation(np.resize(levels, k // 32))).repeat(32)
    a = np.empty((k // 512, 16))
    for p in range(k // 512):
        a[p, :8] = np.random.permutation(np.resize(levels, 8))
        for g in range(8):
            far = levels[np.abs(levels - a[p, g]) >= 10]
            a[p, g + 8] = far[np.random.randint(len(far))]
    return np.exp2(a.ravel()).repeat(32)


def f64(x):
    return np.asarray(x).astype(np.float64)


def striped8(idx):
    return np.concatenate([v.reshape(-1, 16).T for v in idx]).astype(np.uint16)


def unstriped8(offs):
    return np.stack([offs[16 * g:16 * g + 16].T.reshape(-1) for g in range(8)]).astype(np.int64)


E2M1 = np.array([0.0, 0.5, 1.0, 1.5, 2.0, 3.0, 4.0, 6.0, -0.0, -0.5, -1.0, -1.5, -2.0, -3.0, -4.0, -6.0])


def pack_weight(w, fmt):
    k, n = w.shape
    w = f64(np.asarray(w, np.float32).astype(ml_dtypes.bfloat16)).reshape(k // 32, 32, n)
    amax = np.abs(w).max(1)
    if fmt == "e4m3":
        byte = np.frexp(amax)[1] - 1 + 127 - 7
    else:
        mant, ex = np.frexp(amax / 6.0)
        byte = np.where(mant > 0.5, ex, ex - 1) + 127
    byte = np.clip(np.where(amax > 0, byte, 1), 1, 254)
    scaled = (w * np.exp2(127.0 - byte)[:, None, :]).reshape(k, n).astype(np.float32)
    by_word = np.ascontiguousarray(scaled.reshape(k // 512, 128, 4, n).transpose(0, 1, 3, 2))
    if fmt == "e4m3":
        words = by_word.astype(ml_dtypes.float8_e4m3fn).view(np.uint8)
    else:
        c = by_word.astype(ml_dtypes.float4_e2m1fn).view(np.uint8) & 0xF
        words = (c[..., 0::2] | (c[..., 1::2] << 4)).reshape(k // 512, 128, 2 * n)
    return np.ascontiguousarray(words), np.ascontiguousarray(byte.astype(np.uint8).reshape(k // 512, 16, n))


def unpack_weight(words, scales, fmt):
    g, _, n = scales.shape
    words = np.ascontiguousarray(words).reshape(g, 128, n, -1)
    if fmt == "e4m3":
        vals = words.view(ml_dtypes.float8_e4m3fn).astype(np.float64)
    else:
        nib = np.empty((g, 128, n, 4), np.uint8)
        nib[..., 0::2] = words & 0xF
        nib[..., 1::2] = words >> 4
        vals = E2M1[nib]
    vals = vals * np.repeat(np.exp2(scales.astype(np.float64) - 127.0), 8, axis=1)[..., None]
    return vals.transpose(0, 1, 3, 2).reshape(g * 512, n)


K, N, T, J = 1024, 512, 2048, 1024


def setup_inputs():
    n = np.random.standard_normal
    s = mx_kscale(K)[:, None]
    p_wk = pack_weight(n((K, N)) / np.sqrt(K) / s, "e2m1")
    p_wv = pack_weight(n((K, N)) / np.sqrt(K) / s, "e2m1")
    return {
        "xT": (n((K, T)) * s).astype(np.float32),
        "wgt": np.repeat(np.random.uniform(0.5, 2.0, (8, J)), 16, axis=0).astype(np.float32),
        "wk_words": p_wk[0],
        "wk_scales": p_wk[1],
        "wv_words": p_wv[0],
        "wv_scales": p_wv[1],
        "st": (n((N, J))).astype(np.float32),
        "offs": striped8(np.stack([np.random.permutation(T)[:J] for _ in range(8)])),
    }


def reference(xT, wgt, wk_words, wk_scales, wv_words, wv_scales, st, offs):
    idx = unstriped8(offs)
    rows = np.arange(K)
    xg = f64(wgt)[rows // 4 % 128] * f64(xT)[rows[:, None], idx[rows % 512 // 64]]
    xT_ = mxq(xg, 0, "e4m3")
    wk_ = unpack_weight(wk_words, wk_scales, "e2m1")
    wv_ = unpack_weight(wv_words, wv_scales, "e2m1")
    ke = wk_.T @ xT_
    ve = wv_.T @ xT_
    gate = np.tanh(ke * f64(st))
    return gate * ve

@@ -1,0 +1,169 @@
+from contextlib import ExitStack
+
+import concourse.mybir as mybir
+
+K, N, T, J = 1024, 512, 2048, 1024
+FLOPS = 2 * 2 * K * N * J
+
+F32 = mybir.dt.float32
+BF16 = mybir.dt.bfloat16
+I32 = mybir.dt.int32
+U32 = mybir.dt.uint32
+U16 = mybir.dt.uint16
+U8 = mybir.dt.uint8
+FP8X4 = mybir.dt.float8_e4m3fn_x4
+FP4X4 = mybir.dt.float4_e2m1fn_x4
+MULT = mybir.AluOpType.mult
+TANH = mybir.ActivationFunctionType.Tanh
+
+P = 128
+PACK = 4
+PASSES = K // (P * PACK)
+HALF = 512
+HALVES = J // HALF
+ROW_TILES = N // P
+LIST_ROWS = 16
+CHUNKS = ((0, 256), (256, 512), (512, 1024))
+
+
+def tile_list_tanh_kernel(tc, xT, wgt, wk_words, wk_scales, wv_words, wv_scales, st, offs, out):
+    nc = tc.nc
+    with ExitStack() as ctx:
+        held = ctx.enter_context(tc.tile_pool(name="held", bufs=1))
+        ring = ctx.enter_context(tc.tile_pool(name="ring", bufs=3))
+        psum = ctx.enter_context(tc.psum_pool(name="psum", bufs=1))
+
+        offsets = held.tile([P, J // LIST_ROWS], U16, name="offsets")
+        nc.sync.dma_start(offsets[:], offs)
+
+        warm_in = held.tile([P, 8], F32, name="warm_in")
+        warm_out = held.tile([P, 8], F32, name="warm_out")
+        nc.gpsimd.memset(warm_in[:], 0.0)
+        nc.scalar.activation(warm_out[:], warm_in[:], TANH)
+
+        x_rows = xT.rearrange("(a p i) t -> a i p t", a=PASSES, i=PACK)
+        x = {}
+
+        def load_x(a, i):
+            x[a, i] = held.tile([P, T], F32, name=f"x{a}{i}")
+            nc.sync.dma_start(x[a, i][:], x_rows[a, i])
+
+        load_x(0, 0)
+        weight = []
+        for c, (j0, j1) in enumerate(CHUNKS):
+            weight.append(held.tile([P, j1 - j0], F32, name=f"weight{c}"))
+            nc.sync.dma_start(weight[c][:], wgt[:, j0:j1])
+        for a in range(PASSES):
+            for i in range(PACK):
+                if (a, i) != (0, 0):
+                    load_x(a, i)
+
+        sides = (("k", wk_words, wk_scales), ("v", wv_words, wv_scales))
+        w_codes, w_scales = {}, {}
+        for a in range(PASSES):
+            for side, words, scales in sides:
+                w_codes[side, a] = held.tile([P, 2 * N], U8, name=f"w{side}{a}", align_bytes=64)
+                nc.sync.dma_start(w_codes[side, a][:].bitcast(I32), words[a].bitcast(I32))
+        for side, words, scales in sides:
+            w_scales[side] = held.tile([P, PASSES, N], U8, name=f"s{side}", align_bytes=64)
+            nc.gpsimd.memset(w_scales[side][:].rearrange("p a n -> p (a n)").bitcast(I32), 0)
+        for side, words, scales in sides:
+            for q in range(4):
+                nc.gpsimd.dma_start(
+                    w_scales[side][32 * q : 32 * q + 4].bitcast(I32),
+                    scales[:, 4 * q : 4 * q + 4, :].rearrange("a r n -> r a n").bitcast(I32),
+                )
+
+        state = {}
+        for h in range(HALVES):
+            for m in range(ROW_TILES):
+                state[h, m] = held.tile([P, HALF], F32, name=f"state{h}{m}")
+                nc.sync.dma_start(state[h, m][:], st[m * P : (m + 1) * P, h * HALF : (h + 1) * HALF])
+
+        picked = {}
+        rounded = {}
+        x_codes, x_scales = {}, {}
+        for a in range(PASSES):
+            for c, (j0, j1) in enumerate(CHUNKS):
+                picked[a, c] = held.tile([P, PACK, j1 - j0], F32, name=f"picked{a}{c}")
+            for h in range(HALVES):
+                rounded[a, h] = held.tile([P, HALF, PACK], BF16, name=f"rounded{a}{h}", align_bytes=64)
+                x_codes[a, h] = held.tile([P, HALF], U32, name=f"codes{a}{h}", align_bytes=64)
+                x_scales[a, h] = held.tile([P, HALF], U8, name=f"scales{a}{h}", align_bytes=64)
+
+        def gather(a, i, c):
+            j0, j1 = CHUNKS[c]
+            window = x[a, i][:].indirect(offsets[:, j0 // LIST_ROWS : j1 // LIST_ROWS])
+            nc.vector.tensor_tensor(picked[a, c][:, i, :], window, weight[c][:], MULT)
+
+        def interleave(a, c):
+            j0, j1 = CHUNKS[c]
+            h = j0 // HALF
+            nc.scalar.copy(
+                rounded[a, h][:, j0 - h * HALF : j1 - h * HALF, :].rearrange("p (c e) i -> p c i e", e=4),
+                picked[a, c][:].rearrange("p i (c e) -> p c i e", e=4),
+            )
+
+        def quantize(a, h):
+            nc.vector.quantize_mx(
+                out=x_codes[a, h][:].bitcast(FP8X4),
+                scales=x_scales[a, h][:],
+                in_=rounded[a, h][:].rearrange("p j i -> p (j i)"),
+            )
+
+        acc = {}
+
+        def multiply(side, a, h, m):
+            if a == 0:
+                acc[side, h, m] = psum.tile([P, HALF], F32, name=f"acc{side}{m}")
+            nc.tensor.matmul_mx(
+                out=acc[side, h, m][:],
+                lhsT=w_codes[side, a][:, 2 * m * P : 2 * (m + 1) * P].bitcast(FP4X4),
+                lhsT_scale=w_scales[side][:, a, m * P : (m + 1) * P],
+                rhs=x_codes[a, h][:].bitcast(FP8X4),
+                rhs_scale=x_scales[a, h][:],
+                start=(a == 0),
+                stop=(a == PASSES - 1),
+            )
+
+        for a in range(PASSES):
+            for i in range(PACK):
+                for c in range(len(CHUNKS)):
+                    gather(a, i, c)
+                    if i == PACK - 1:
+                        interleave(a, c)
+                if (a, i) == (1, 1):
+                    quantize(0, 0)
+        quantize(0, 1)
+        for m in range(ROW_TILES):
+            multiply("k", 0, 0, m)
+            multiply("v", 0, 0, m)
+        quantize(1, 0)
+        for m in range(ROW_TILES):
+            multiply("k", 1, 0, m)
+            multiply("v", 1, 0, m)
+        quantize(1, 1)
+
+        steps = [(h, m) for h in range(HALVES) for m in range(ROW_TILES)]
+        gates = {}
+
+        def gate(h, m):
+            pre = ring.tile([P, HALF], F32, name="pre")
+            nc.vector.tensor_tensor(pre[:], acc["k", h, m][:], state[h, m][:], MULT)
+            gates[h, m] = ring.tile([P, HALF], F32, name="gate")
+            nc.scalar.activation(gates[h, m][:], pre[:], TANH)
+
+        def finish(h, m):
+            result = held.tile([P, HALF], F32, name=f"result{h}{m}")
+            nc.vector.tensor_tensor(result[:], acc["v", h, m][:], gates[h, m][:], MULT)
+            nc.sync.dma_start(out[m * P : (m + 1) * P, h * HALF : (h + 1) * HALF], result[:])
+            if h + 1 < HALVES:
+                for side in ("k", "v"):
+                    for a in range(PASSES):
+                        multiply(side, a, h + 1, m)
+
+        for s, (h, m) in enumerate(steps):
+            gate(h, m)
+            if s > 0:
+                finish(*steps[s - 1])
+        finish(*steps[-1])

@@ -23,23 +23,17 @@ HALF = 512
 HALVES = J // HALF
 ROW_TILES = N // P
 LIST_ROWS = 16
+FIRST = 256
 CHUNKS = ((0, 256), (256, 512), (512, 1024))
+LAST_PIECES = 2
+GPSIMD_TILES = 3
 
 
 def tile_list_tanh_kernel(tc, xT, wgt, wk_words, wk_scales, wv_words, wv_scales, st, offs, out):
     nc = tc.nc
     with ExitStack() as ctx:
         held = ctx.enter_context(tc.tile_pool(name="held", bufs=1))
-        ring = ctx.enter_context(tc.tile_pool(name="ring", bufs=3))
         psum = ctx.enter_context(tc.psum_pool(name="psum", bufs=1))
-
-        offsets = held.tile([P, J // LIST_ROWS], U16, name="offsets")
-        nc.sync.dma_start(offsets[:], offs)
-
-        warm_in = held.tile([P, 8], F32, name="warm_in")
-        warm_out = held.tile([P, 8], F32, name="warm_out")
-        nc.gpsimd.memset(warm_in[:], 0.0)
-        nc.scalar.activation(warm_out[:], warm_in[:], TANH)
 
         x_rows = xT.rearrange("(a p i) t -> a i p t", a=PASSES, i=PACK)
         x = {}
@@ -48,63 +42,70 @@ def tile_list_tanh_kernel(tc, xT, wgt, wk_words, wk_scales, wv_words, wv_scales,
             x[a, i] = held.tile([P, T], F32, name=f"x{a}{i}")
             nc.sync.dma_start(x[a, i][:], x_rows[a, i])
 
+        offsets = held.tile([P, J // LIST_ROWS], U16, name="offsets")
+        weight = held.tile([P, J], F32, name="weight")
         load_x(0, 0)
-        weight = []
-        for c, (j0, j1) in enumerate(CHUNKS):
-            weight.append(held.tile([P, j1 - j0], F32, name=f"weight{c}"))
-            nc.sync.dma_start(weight[c][:], wgt[:, j0:j1])
-        for a in range(PASSES):
-            for i in range(PACK):
-                if (a, i) != (0, 0):
-                    load_x(a, i)
-
+        nc.sync.dma_start(offsets[:], offs)
+        nc.sync.dma_start(weight[:, :FIRST], wgt[:, :FIRST])
+        nc.sync.dma_start(weight[:, FIRST:], wgt[:, FIRST:])
         sides = (("k", wk_words, wk_scales), ("v", wv_words, wv_scales))
         w_codes, w_scales = {}, {}
+        for side, words, scales in sides:
+            w_scales[side] = held.tile([P, PASSES, N], U8, name=f"s{side}", align_bytes=64)
+            nc.gpsimd.memset(w_scales[side][:].rearrange("p a n -> p (a n)").bitcast(I32), 0)
+        for i in range(1, PACK):
+            load_x(0, i)
+        load_x(1, 0)
+        load_x(1, 1)
+        for (side, words, scales), i in zip(sides, (2, 3)):
+            for q in range(4):
+                nc.sync.dma_start(
+                    w_scales[side][32 * q : 32 * q + 4].bitcast(I32),
+                    scales[:, 4 * q : 4 * q + 4, :].rearrange("a r n -> r a n").bitcast(I32),
+                )
+            load_x(1, i)
+
         for a in range(PASSES):
             for side, words, scales in sides:
                 w_codes[side, a] = held.tile([P, 2 * N], U8, name=f"w{side}{a}", align_bytes=64)
                 nc.sync.dma_start(w_codes[side, a][:].bitcast(I32), words[a].bitcast(I32))
-        for side, words, scales in sides:
-            w_scales[side] = held.tile([P, PASSES, N], U8, name=f"s{side}", align_bytes=64)
-            nc.gpsimd.memset(w_scales[side][:].rearrange("p a n -> p (a n)").bitcast(I32), 0)
-        for side, words, scales in sides:
-            for q in range(4):
-                nc.gpsimd.dma_start(
-                    w_scales[side][32 * q : 32 * q + 4].bitcast(I32),
-                    scales[:, 4 * q : 4 * q + 4, :].rearrange("a r n -> r a n").bitcast(I32),
-                )
 
         state = {}
         for h in range(HALVES):
             for m in range(ROW_TILES):
-                state[h, m] = held.tile([P, HALF], F32, name=f"state{h}{m}")
+                state[h, m] = held.tile([P, HALF], F32, name=f"state{h}{m}", align_bytes=64)
                 nc.sync.dma_start(state[h, m][:], st[m * P : (m + 1) * P, h * HALF : (h + 1) * HALF])
 
-        picked = {}
         rounded = {}
         x_codes, x_scales = {}, {}
         for a in range(PASSES):
-            for c, (j0, j1) in enumerate(CHUNKS):
-                picked[a, c] = held.tile([P, PACK, j1 - j0], F32, name=f"picked{a}{c}")
             for h in range(HALVES):
                 rounded[a, h] = held.tile([P, HALF, PACK], BF16, name=f"rounded{a}{h}", align_bytes=64)
-                x_codes[a, h] = held.tile([P, HALF], U32, name=f"codes{a}{h}", align_bytes=64)
-                x_scales[a, h] = held.tile([P, HALF], U8, name=f"scales{a}{h}", align_bytes=64)
 
-        def gather(a, i, c):
-            j0, j1 = CHUNKS[c]
+        first_pass = held.tile([P, PACK, J], F32, name="first_pass")
+        early_pair = held.tile([P, 2, J], F32, name="early_pair")
+        late_pair = [held.tile([P, 2, j1 - j0], F32, name=f"late_pair{j0}") for j0, j1 in CHUNKS]
+
+        def gather(dest, a, i, j0, j1):
             window = x[a, i][:].indirect(offsets[:, j0 // LIST_ROWS : j1 // LIST_ROWS])
-            nc.vector.tensor_tensor(picked[a, c][:, i, :], window, weight[c][:], MULT)
+            nc.vector.tensor_tensor(dest, window, weight[:, j0:j1], MULT)
 
-        def interleave(a, c):
-            j0, j1 = CHUNKS[c]
-            h = j0 // HALF
+        def interleave_four(a, h):
             nc.scalar.copy(
-                rounded[a, h][:, j0 - h * HALF : j1 - h * HALF, :].rearrange("p (c e) i -> p c i e", e=4),
-                picked[a, c][:].rearrange("p i (c e) -> p c i e", e=4),
+                rounded[a, h][:].rearrange("p (c e) i -> p c i e", e=4),
+                first_pass[:, :, h * HALF : (h + 1) * HALF].rearrange("p i (c e) -> p c i e", e=4),
             )
 
-        def quantize(a, h):
+        def interleave_two(src, a, i0, j0, j1):
+            h = j0 // HALF
+            nc.scalar.copy(
+                rounded[a, h][:, j0 - h * HALF : j1 - h * HALF, i0 : i0 + 2],
+                src.rearrange("p i j -> p j i"),
+            )
+
+        def quantize(a, h, tag):
+            x_codes[a, h] = held.tile([P, HALF], U32, name=f"codes{a}{h}", tag=tag, align_bytes=64)
+            x_scales[a, h] = held.tile([P, HALF], U8, name=f"scales{a}{h}", align_bytes=64)
             nc.vector.quantize_mx(
                 out=x_codes[a, h][:].bitcast(FP8X4),
                 scales=x_scales[a, h][:],
@@ -126,44 +127,72 @@ def tile_list_tanh_kernel(tc, xT, wgt, wk_words, wk_scales, wv_words, wv_scales,
                 stop=(a == PASSES - 1),
             )
 
-        for a in range(PASSES):
-            for i in range(PACK):
-                for c in range(len(CHUNKS)):
-                    gather(a, i, c)
-                    if i == PACK - 1:
-                        interleave(a, c)
-                if (a, i) == (1, 1):
-                    quantize(0, 0)
-        quantize(0, 1)
+        gather(first_pass[:, 0, :FIRST], 0, 0, 0, FIRST)
+        gather(first_pass[:, 0, FIRST:], 0, 0, FIRST, J)
+        for i in range(1, PACK):
+            gather(first_pass[:, i, :], 0, i, 0, J)
+        for h in range(HALVES):
+            interleave_four(0, h)
+        gather(early_pair[:, 0, :], 1, 0, 0, J)
+        gather(early_pair[:, 1, :], 1, 1, 0, J)
+        quantize(0, 0, "codes00")
+        for h in range(HALVES):
+            interleave_two(early_pair[:, :, h * HALF : (h + 1) * HALF], 1, 0, h * HALF, (h + 1) * HALF)
+        for c, (j0, j1) in enumerate(CHUNKS):
+            gather(late_pair[c][:, 0, :], 1, 2, j0, j1)
+        for c, (j0, j1) in enumerate(CHUNKS):
+            gather(late_pair[c][:, 1, :], 1, 3, j0, j1)
+            interleave_two(late_pair[c][:], 1, 2, j0, j1)
         for m in range(ROW_TILES):
             multiply("k", 0, 0, m)
             multiply("v", 0, 0, m)
-        quantize(1, 0)
+        quantize(1, 0, "codes10")
+        quantize(0, 1, "rounded10")
         for m in range(ROW_TILES):
             multiply("k", 1, 0, m)
             multiply("v", 1, 0, m)
-        quantize(1, 1)
 
-        steps = [(h, m) for h in range(HALVES) for m in range(ROW_TILES)]
-        gates = {}
-
-        def gate(h, m):
-            pre = ring.tile([P, HALF], F32, name="pre")
+        def gate(h, m, pieces):
+            pre = held.tile([P, HALF], F32, name=f"pre{h}{m}")
             nc.vector.tensor_tensor(pre[:], acc["k", h, m][:], state[h, m][:], MULT)
-            gates[h, m] = ring.tile([P, HALF], F32, name="gate")
-            nc.scalar.activation(gates[h, m][:], pre[:], TANH)
+            gated = held.tile([P, HALF], F32, name=f"gate{h}{m}")
+            for cols in pieces:
+                nc.scalar.activation(gated[:, cols], pre[:, cols], TANH)
+            return gated
 
-        def finish(h, m):
+        def store(result, h, m, cols):
+            nc.sync.dma_start(out[m * P : (m + 1) * P, h * HALF + cols.start : h * HALF + cols.stop], result[:, cols])
+
+        whole = [slice(0, HALF)]
+        width = HALF // LAST_PIECES
+        steps = [(h, m) for h in range(HALVES) for m in range(ROW_TILES)]
+        pieces = {step: whole for step in steps}
+        pieces[steps[-1]] = [slice(c * width, (c + 1) * width) for c in range(LAST_PIECES)]
+        values, gates = {}, {}
+
+        def finish(engine, h, m):
             result = held.tile([P, HALF], F32, name=f"result{h}{m}")
-            nc.vector.tensor_tensor(result[:], acc["v", h, m][:], gates[h, m][:], MULT)
-            nc.sync.dma_start(out[m * P : (m + 1) * P, h * HALF : (h + 1) * HALF], result[:])
-            if h + 1 < HALVES:
-                for side in ("k", "v"):
-                    for a in range(PASSES):
-                        multiply(side, a, h + 1, m)
+            for cols in pieces[h, m]:
+                engine.tensor_tensor(result[:, cols], values[h, m][:, cols], gates[h, m][:, cols], MULT)
+                store(result, h, m, cols)
 
-        for s, (h, m) in enumerate(steps):
-            gate(h, m)
-            if s > 0:
-                finish(*steps[s - 1])
-        finish(*steps[-1])
+        for m in range(ROW_TILES):
+            values[0, m] = acc["v", 0, m]
+            if m < GPSIMD_TILES:
+                values[0, m] = held.tile([P, HALF], F32, name=f"values{m}")
+                nc.scalar.copy(values[0, m][:], acc["v", 0, m][:])
+            gates[0, m] = gate(0, m, whole)
+            finish(nc.gpsimd if m < GPSIMD_TILES else nc.vector, 0, m)
+            if m == 0:
+                quantize(1, 1, "state00")
+            for a in range(PASSES):
+                multiply("k", a, 1, m)
+        for m in range(ROW_TILES):
+            for a in range(PASSES):
+                multiply("v", a, 1, m)
+            values[1, m] = acc["v", 1, m]
+        for m in range(ROW_TILES):
+            gates[1, m] = gate(1, m, pieces[1, m])
+            if m > 0:
+                finish(nc.vector, 1, m - 1)
+        finish(nc.vector, 1, ROW_TILES - 1)

@@ -1,6 +1,7 @@
 from contextlib import ExitStack
 
 import concourse.mybir as mybir
+from concourse.masks import make_identity
 
 K, N, T, J = 1024, 512, 2048, 1024
 FLOPS = 2 * 2 * K * N * J
@@ -43,11 +44,29 @@ def tile_list_tanh_kernel(tc, xT, wgt, wk_words, wk_scales, wv_words, wv_scales,
             nc.sync.dma_start(x[a, i][:], x_rows[a, i])
 
         offsets = held.tile([P, J // LIST_ROWS], U16, name="offsets")
-        weight = held.tile([P, J], F32, name="weight")
+        compact = held.tile([P, P], F32, name="compact")
+        two_rows = wgt.rearrange("(g s) (r c) -> g s r c", s=LIST_ROWS, c=P)[:, 0:2]
+        nc.sync.dma_start(compact[:], two_rows.rearrange("g u r c -> g (u r) c"))
         load_x(0, 0)
         nc.sync.dma_start(offsets[:], offs)
-        nc.sync.dma_start(weight[:, :FIRST], wgt[:, :FIRST])
-        nc.sync.dma_start(weight[:, FIRST:], wgt[:, FIRST:])
+
+        identity = held.tile([P, P], F32, name="identity")
+        make_identity(nc, identity[:])
+        turned = psum.tile([P, P], F32, name="acck0")
+        nc.tensor.transpose(turned[:], compact[:], identity[:])
+        weight = held.tile([P, J], F32, name="weight")
+        by_block = turned[:].rearrange("c (s r) -> c r s", r=J // P)
+        for piece in range(J // FIRST):
+            blocks = FIRST // P
+            spread = held.tile([P, blocks, LIST_ROWS, 8], F32, name=f"spread{piece}")
+            nc.vector.tensor_copy(
+                spread[:],
+                by_block[:, piece * blocks : (piece + 1) * blocks, :].unsqueeze(3).to_broadcast([P, blocks, LIST_ROWS, 8]),
+            )
+            back = psum.tile([P, FIRST], F32, name=f"accv{piece}")
+            for b in range(blocks):
+                nc.tensor.transpose(back[:, b * P : (b + 1) * P], spread[:, b].rearrange("c s e -> c (s e)"), identity[:])
+            nc.scalar.copy(weight[:, piece * FIRST : (piece + 1) * FIRST], back[:])
         sides = (("k", wk_words, wk_scales), ("v", wv_words, wv_scales))
         w_codes, w_scales = {}, {}
         for side, words, scales in sides:
@@ -127,8 +146,8 @@ def tile_list_tanh_kernel(tc, xT, wgt, wk_words, wk_scales, wv_words, wv_scales,
                 stop=(a == PASSES - 1),
             )
 
-        gather(first_pass[:, 0, :FIRST], 0, 0, 0, FIRST)
-        gather(first_pass[:, 0, FIRST:], 0, 0, FIRST, J)
+        for j0, j1 in CHUNKS:
+            gather(first_pass[:, 0, j0:j1], 0, 0, j0, j1)
         for i in range(1, PACK):
             gather(first_pass[:, i, :], 0, i, 0, J)
         for h in range(HALVES):

@@ -84,16 +84,17 @@ def tile_list_tanh_kernel(tc, xT, wgt, wk_words, wk_scales, wv_words, wv_scales,
                 )
             load_x(1, i)
 
-        for a in range(PASSES):
-            for side, words, scales in sides:
-                w_codes[side, a] = held.tile([P, 2 * N], U8, name=f"w{side}{a}", align_bytes=64)
-                nc.sync.dma_start(w_codes[side, a][:].bitcast(I32), words[a].bitcast(I32))
 
         state = {}
         for h in range(HALVES):
             for m in range(ROW_TILES):
                 state[h, m] = held.tile([P, HALF], F32, name=f"state{h}{m}", align_bytes=64)
                 nc.sync.dma_start(state[h, m][:], st[m * P : (m + 1) * P, h * HALF : (h + 1) * HALF])
+                if (h, m) == (0, 1):
+                    for a in range(PASSES):
+                        for side, words, scales in sides:
+                            w_codes[side, a] = held.tile([P, 2 * N], U8, name=f"w{side}{a}", align_bytes=64)
+                            nc.sync.dma_start(w_codes[side, a][:].bitcast(I32), words[a].bitcast(I32))
 
         rounded = {}
         x_codes, x_scales = {}, {}
@@ -186,7 +187,8 @@ def tile_list_tanh_kernel(tc, xT, wgt, wk_words, wk_scales, wv_words, wv_scales,
         width = HALF // LAST_PIECES
         steps = [(h, m) for h in range(HALVES) for m in range(ROW_TILES)]
         pieces = {step: whole for step in steps}
-        pieces[steps[-1]] = [slice(c * width, (c + 1) * width) for c in range(LAST_PIECES)]
+        for step in steps[-2:]:
+            pieces[step] = [slice(c * width, (c + 1) * width) for c in range(LAST_PIECES)]
         values, gates = {}, {}
 
         def finish(engine, h, m):
@@ -211,7 +213,7 @@ def tile_list_tanh_kernel(tc, xT, wgt, wk_words, wk_scales, wv_words, wv_scales,
                 multiply("v", a, 1, m)
             values[1, m] = acc["v", 1, m]
         for m in range(ROW_TILES):
-            gates[1, m] = gate(1, m, pieces[1, m])
+            gates[1, m] = gate(1, m, pieces[1, m] if m == ROW_TILES - 1 else whole)
             if m > 0:
                 finish(nc.vector, 1, m - 1)
         finish(nc.vector, 1, ROW_TILES - 1)

from contextlib import ExitStack

import concourse.mybir as mybir
from concourse.masks import make_identity

K, N, T, J = 1024, 512, 2048, 1024
FLOPS = 2 * 2 * K * N * J

F32 = mybir.dt.float32
BF16 = mybir.dt.bfloat16
I32 = mybir.dt.int32
U32 = mybir.dt.uint32
U16 = mybir.dt.uint16
U8 = mybir.dt.uint8
FP8X4 = mybir.dt.float8_e4m3fn_x4
FP4X4 = mybir.dt.float4_e2m1fn_x4
MULT = mybir.AluOpType.mult
TANH = mybir.ActivationFunctionType.Tanh

P = 128
PACK = 4
PASSES = K // (P * PACK)
HALF = 512
HALVES = J // HALF
ROW_TILES = N // P
LIST_ROWS = 16
FIRST = 256
CHUNKS = ((0, 256), (256, 512), (512, 1024))
LAST_PIECES = 2
GPSIMD_TILES = 3


def tile_list_tanh_kernel(tc, xT, wgt, wk_words, wk_scales, wv_words, wv_scales, st, offs, out):
    nc = tc.nc
    with ExitStack() as ctx:
        held = ctx.enter_context(tc.tile_pool(name="held", bufs=1))
        psum = ctx.enter_context(tc.psum_pool(name="psum", bufs=1))

        x_rows = xT.rearrange("(a p i) t -> a i p t", a=PASSES, i=PACK)
        x = {}

        def load_x(a, i):
            x[a, i] = held.tile([P, T], F32, name=f"x{a}{i}")
            nc.sync.dma_start(x[a, i][:], x_rows[a, i])

        offsets = held.tile([P, J // LIST_ROWS], U16, name="offsets")
        compact = held.tile([P, P], F32, name="compact")
        two_rows = wgt.rearrange("(g s) (r c) -> g s r c", s=LIST_ROWS, c=P)[:, 0:2]
        nc.sync.dma_start(compact[:], two_rows.rearrange("g u r c -> g (u r) c"))
        load_x(0, 0)
        nc.sync.dma_start(offsets[:], offs)

        identity = held.tile([P, P], F32, name="identity")
        make_identity(nc, identity[:])
        turned = psum.tile([P, P], F32, name="acck0")
        nc.tensor.transpose(turned[:], compact[:], identity[:])
        weight = held.tile([P, J], F32, name="weight")
        by_block = turned[:].rearrange("c (s r) -> c r s", r=J // P)
        for piece in range(J // FIRST):
            blocks = FIRST // P
            spread = held.tile([P, blocks, LIST_ROWS, 8], F32, name=f"spread{piece}")
            nc.vector.tensor_copy(
                spread[:],
                by_block[:, piece * blocks : (piece + 1) * blocks, :].unsqueeze(3).to_broadcast([P, blocks, LIST_ROWS, 8]),
            )
            back = psum.tile([P, FIRST], F32, name=f"accv{piece}")
            for b in range(blocks):
                nc.tensor.transpose(back[:, b * P : (b + 1) * P], spread[:, b].rearrange("c s e -> c (s e)"), identity[:])
            nc.scalar.copy(weight[:, piece * FIRST : (piece + 1) * FIRST], back[:])
        sides = (("k", wk_words, wk_scales), ("v", wv_words, wv_scales))
        w_codes, w_scales = {}, {}
        for side, words, scales in sides:
            w_scales[side] = held.tile([P, PASSES, N], U8, name=f"s{side}", align_bytes=64)
            nc.gpsimd.memset(w_scales[side][:].rearrange("p a n -> p (a n)").bitcast(I32), 0)
        for i in range(1, PACK):
            load_x(0, i)
        load_x(1, 0)
        load_x(1, 1)
        for (side, words, scales), i in zip(sides, (2, 3)):
            for q in range(4):
                nc.sync.dma_start(
                    w_scales[side][32 * q : 32 * q + 4].bitcast(I32),
                    scales[:, 4 * q : 4 * q + 4, :].rearrange("a r n -> r a n").bitcast(I32),
                )
            load_x(1, i)


        state = {}
        for h in range(HALVES):
            for m in range(ROW_TILES):
                state[h, m] = held.tile([P, HALF], F32, name=f"state{h}{m}", align_bytes=64)
                nc.sync.dma_start(state[h, m][:], st[m * P : (m + 1) * P, h * HALF : (h + 1) * HALF])
                if (h, m) == (0, 1):
                    for a in range(PASSES):
                        for side, words, scales in sides:
                            w_codes[side, a] = held.tile([P, 2 * N], U8, name=f"w{side}{a}", align_bytes=64)
                            nc.sync.dma_start(w_codes[side, a][:].bitcast(I32), words[a].bitcast(I32))

        rounded = {}
        x_codes, x_scales = {}, {}
        for a in range(PASSES):
            for h in range(HALVES):
                rounded[a, h] = held.tile([P, HALF, PACK], BF16, name=f"rounded{a}{h}", align_bytes=64)

        first_pass = held.tile([P, PACK, J], F32, name="first_pass")
        early_pair = held.tile([P, 2, J], F32, name="early_pair")
        late_pair = [held.tile([P, 2, j1 - j0], F32, name=f"late_pair{j0}") for j0, j1 in CHUNKS]

        def gather(dest, a, i, j0, j1):
            window = x[a, i][:].indirect(offsets[:, j0 // LIST_ROWS : j1 // LIST_ROWS])
            nc.vector.tensor_tensor(dest, window, weight[:, j0:j1], MULT)

        def interleave_four(a, h):
            nc.scalar.copy(
                rounded[a, h][:].rearrange("p (c e) i -> p c i e", e=4),
                first_pass[:, :, h * HALF : (h + 1) * HALF].rearrange("p i (c e) -> p c i e", e=4),
            )

        def interleave_two(src, a, i0, j0, j1):
            h = j0 // HALF
            nc.scalar.copy(
                rounded[a, h][:, j0 - h * HALF : j1 - h * HALF, i0 : i0 + 2],
                src.rearrange("p i j -> p j i"),
            )

        def quantize(a, h, tag):
            x_codes[a, h] = held.tile([P, HALF], U32, name=f"codes{a}{h}", tag=tag, align_bytes=64)
            x_scales[a, h] = held.tile([P, HALF], U8, name=f"scales{a}{h}", align_bytes=64)
            nc.vector.quantize_mx(
                out=x_codes[a, h][:].bitcast(FP8X4),
                scales=x_scales[a, h][:],
                in_=rounded[a, h][:].rearrange("p j i -> p (j i)"),
            )

        acc = {}

        def multiply(side, a, h, m):
            if a == 0:
                acc[side, h, m] = psum.tile([P, HALF], F32, name=f"acc{side}{m}")
            nc.tensor.matmul_mx(
                out=acc[side, h, m][:],
                lhsT=w_codes[side, a][:, 2 * m * P : 2 * (m + 1) * P].bitcast(FP4X4),
                lhsT_scale=w_scales[side][:, a, m * P : (m + 1) * P],
                rhs=x_codes[a, h][:].bitcast(FP8X4),
                rhs_scale=x_scales[a, h][:],
                start=(a == 0),
                stop=(a == PASSES - 1),
            )

        for j0, j1 in CHUNKS:
            gather(first_pass[:, 0, j0:j1], 0, 0, j0, j1)
        for i in range(1, PACK):
            gather(first_pass[:, i, :], 0, i, 0, J)
        for h in range(HALVES):
            interleave_four(0, h)
        gather(early_pair[:, 0, :], 1, 0, 0, J)
        gather(early_pair[:, 1, :], 1, 1, 0, J)
        quantize(0, 0, "codes00")
        for h in range(HALVES):
            interleave_two(early_pair[:, :, h * HALF : (h + 1) * HALF], 1, 0, h * HALF, (h + 1) * HALF)
        for c, (j0, j1) in enumerate(CHUNKS):
            gather(late_pair[c][:, 0, :], 1, 2, j0, j1)
        for c, (j0, j1) in enumerate(CHUNKS):
            gather(late_pair[c][:, 1, :], 1, 3, j0, j1)
            interleave_two(late_pair[c][:], 1, 2, j0, j1)
        for m in range(ROW_TILES):
            multiply("k", 0, 0, m)
            multiply("v", 0, 0, m)
        quantize(1, 0, "codes10")
        quantize(0, 1, "rounded10")
        for m in range(ROW_TILES):
            multiply("k", 1, 0, m)
            multiply("v", 1, 0, m)

        def gate(h, m, pieces):
            pre = held.tile([P, HALF], F32, name=f"pre{h}{m}")
            nc.vector.tensor_tensor(pre[:], acc["k", h, m][:], state[h, m][:], MULT)
            gated = held.tile([P, HALF], F32, name=f"gate{h}{m}")
            for cols in pieces:
                nc.scalar.activation(gated[:, cols], pre[:, cols], TANH)
            return gated

        def store(result, h, m, cols):
            nc.sync.dma_start(out[m * P : (m + 1) * P, h * HALF + cols.start : h * HALF + cols.stop], result[:, cols])

        whole = [slice(0, HALF)]
        width = HALF // LAST_PIECES
        steps = [(h, m) for h in range(HALVES) for m in range(ROW_TILES)]
        pieces = {step: whole for step in steps}
        for step in steps[-2:]:
            pieces[step] = [slice(c * width, (c + 1) * width) for c in range(LAST_PIECES)]
        values, gates = {}, {}

        def finish(engine, h, m):
            result = held.tile([P, HALF], F32, name=f"result{h}{m}")
            for cols in pieces[h, m]:
                engine.tensor_tensor(result[:, cols], values[h, m][:, cols], gates[h, m][:, cols], MULT)
                store(result, h, m, cols)

        for m in range(ROW_TILES):
            values[0, m] = acc["v", 0, m]
            if m < GPSIMD_TILES:
                values[0, m] = held.tile([P, HALF], F32, name=f"values{m}")
                nc.scalar.copy(values[0, m][:], acc["v", 0, m][:])
            gates[0, m] = gate(0, m, whole)
            finish(nc.gpsimd if m < GPSIMD_TILES else nc.vector, 0, m)
            if m == 0:
                quantize(1, 1, "state00")
            for a in range(PASSES):
                multiply("k", a, 1, m)
        for m in range(ROW_TILES):
            for a in range(PASSES):
                multiply("v", a, 1, m)
            values[1, m] = acc["v", 1, m]
        for m in range(ROW_TILES):
            gates[1, m] = gate(1, m, pieces[1, m] if m == ROW_TILES - 1 else whole)
            if m > 0:
                finish(nc.vector, 1, m - 1)
        finish(nc.vector, 1, ROW_TILES - 1)
